import numpy as np, ml_dtypes
CORES = [10,34,74,98]
N = 4
BF = ml_dtypes.bfloat16
def gentries(a):
    return np.ascontiguousarray(a.reshape(8, 16, -1).transpose(0, 2, 1)).reshape(8, -1)
def gtable(e):
    e = np.asarray(e); return np.ascontiguousarray(e.reshape(8, -1, 16).transpose(0, 2, 1)).reshape(128, -1).astype(np.int32)
K, D, SH = 1024, 4096, 4
def sized(rng):
    return rng.standard_normal((N, 128, D), dtype=np.float32) * np.exp2(rng.integers(-1, 2, (N, 128, 1))).astype(np.float32)
def hashes(a, b):
    return np.repeat(np.stack([a, b], 2), 16, axis=1).astype(np.int32)
def lists(e):
    return np.stack([gtable(u) for u in e])
def setup_inputs(rng):
    a = np.stack([rng.permutation(255)[:8] + 1 for r in range(N)]); b = rng.integers(0, 65536, (N, 8))
    return {"mat": sized(rng).astype(BF), "ids": lists(rng.integers(0, 65536, (N, 8, K))), "hs": hashes(a, b)}
def setup_inputs_ends(rng):
    e = rng.integers(0, 65536, (N, 8, K)); e = np.where(rng.random(e.shape) < 0.5, rng.choice(np.array([0, 1, 65534, 65535]), e.shape), e)
    e[:, :, 0] = 0; e[:, :, 1] = 1 << SH; e[:, :, -1] = 65535
    top = (D - 1) << SH; low = (1 << SH) - 1
    a = rng.choice(np.array([0, 1, 254, 255]), (N, 8)); b = rng.choice(np.array([0, 1, low, top, top + low, 65535]), (N, 8))
    for r in range(N):
        a[r, r % 8], b[r, r % 8] = 1, top
        a[r, (r + 1) % 8], b[r, (r + 1) % 8] = 255, 65535
        a[r, (r + 2) % 8] = 0
        a[r, (r + 3) % 8], b[r, (r + 3) % 8] = 1, top + low
    return {"mat": sized(rng).astype(BF), "ids": lists(e), "hs": hashes(a, b)}
def setup_inputs_one(rng):
    d = setup_inputs(rng); e = rng.integers(0, 65536, (N, 8, K)); o = rng.permutation(N)
    e[o[0]] = rng.permutation(65536)[:8, None]; e[o[1]] = e[o[2]]; e[o[3]] = np.repeat(e[o[3], :, :K // 16], 16, axis=1)
    d["ids"] = lists(e); d["hs"][rng.integers(0, N), :, 0] = 0; return d
def setup_inputs_turns(rng):
    d = setup_inputs(rng); p = np.argsort(rng.random((N, 8, D, 4)), axis=3)
    w = (rng.integers(128, 256, p.shape) * (2 * rng.integers(0, 2, p.shape) - 1)).astype(np.float32) * np.float32(2.0 ** -7)
    m = np.where(p[..., None] == np.arange(4), w[..., None], np.float32(0))
    d["mat"] = np.ascontiguousarray(m.transpose(0, 1, 3, 4, 2)).reshape(N, 128, D).astype(BF); return d
def setup_inputs_spread(rng):
    d = setup_inputs(rng); k = (N, 8, 1, D)
    z = (np.exp2(rng.integers(-2, 3, k)) * (rng.random(k) > 0.03125)).astype(np.float32)
    d["mat"] = (sized(rng).reshape(N, 8, 16, D) * z).reshape(N, 128, D).astype(BF); return d
def check_inputs(d):
    bad = []; h = d["hs"].reshape(N, 8, 16, 2)
    if not (np.abs(d["mat"].astype(np.float32)) <= 8192).all(): bad.append("size of mat")
    if not ((d["ids"] >= 0) & (d["ids"] <= 65535)).all(): bad.append("range of ids")
    if not ((h >= 0) & (h <= np.array([255, 65535]))).all(): bad.append("range of hs")
    if not (h == h[:, :, :1]).all(): bad.append("rows of hs alike in a group")
    return bad
def reference(mat, ids, hs):
    y = np.zeros((N, 32, K), np.float64); m = mat.astype(np.float64).reshape(N, 8, 16, D); h = hs.astype(np.int64)[:, ::16]
    for r in range(N):
        i = gentries(ids[r]).astype(np.int64)
        v = np.zeros((8, 4, K), np.float64); v[:, 0] = 1
        for q in range(N):
            t = ((i * h[q, :, :1] + h[q, :, 1:]) >> SH) & (D - 1)
            x = np.take_along_axis(m[q], t[:, None, :], 2).reshape(8, 4, 4, K)
            v = np.sum(v[:, :, None, :] * x, axis=1)
        y[r] = v.reshape(32, K)
    return {"y": y.astype(np.float32)}

@@ -1,0 +1,265 @@
+from concourse.mybir import AluOpType, ActivationFunctionType
+
+N = 4
+K = 1024
+H = K // 2
+L = K // 16
+A = AluOpType
+
+SCRATCH = {
+    "idl": ("sbuf", [128, N * L], "int32"),
+    "hsi": ("sbuf", [128, 2], "int32"),
+    "hsf": ("sbuf", [128, 2], "float32"),
+    "win": ("sbuf", [128, 4096], "bfloat16"),
+    "t1": ("sbuf", [128, N * L], "int32"),
+    "t2": ("sbuf", [128, N * L], "int32"),
+    "offs": ("sbuf", [128, N * L], "uint16"),
+    "gat": ("sbuf", [128, N * K], "bfloat16"),
+    "land": ("sbuf", [128, N * K], "bfloat16"),
+    "c0s": ("sbuf", [128, N * 256], "bfloat16"),
+    "c0l": ("sbuf", [128, 256], "bfloat16"),
+    "hi": ("sbuf", [128, K], "bfloat16"),
+    "lo": ("sbuf", [128, K], "bfloat16"),
+    "p2": ("sbuf", [128, K], "float32"),
+    "p3": ("sbuf", [128, K], "float32"),
+    "yb": ("sbuf", [128, K], "float32"),
+    "km": ("sbuf", [128, 128], "float32"),
+    "m32": ("sbuf", [128, 32], "float32"),
+    "pidx": ("sbuf", [128, 1], "int32"),
+    "i1": ("sbuf", [128, 1], "int32"),
+    "i2": ("sbuf", [128, 1], "int32"),
+    "i3": ("sbuf", [128, 1], "int32"),
+    "keyp": ("sbuf", [128, 1], "float32"),
+    "key0": ("sbuf", [128, 1], "float32"),
+    "sf": ("sbuf", [128, 128], "float32"),
+    "sb": ("sbuf", [128, 128], "bfloat16"),
+    "so": ("sbuf", [128, 32], "float32"),
+    "ex": ("sbuf", [128, 512], "bfloat16"),
+    "cm": ("sbuf", [128, 512], "bfloat16"),
+    "pv00": ("psum", [128, H], "float32"),
+    "pv01": ("psum", [128, H], "float32"),
+    "pv10": ("psum", [128, H], "float32"),
+    "pv11": ("psum", [128, H], "float32"),
+    "pv20": ("psum", [128, H], "float32"),
+    "pv21": ("psum", [128, H], "float32"),
+    "pp0": ("psum", [128, H], "float32"),
+    "pp1": ("psum", [128, H], "float32"),
+}
+SEMAPHORES = (["e%d" % i for i in range(100)] + ["ida%d" % r for r in range(N)]
+              + ["ma%d_%d" % (q, h) for q in range(1, N) for h in range(2)] + ["va", "ls"])
+
+IDS_TO = {0: [1, 2, 3], 1: [0, 3, 2], 2: [3, 0, 1], 3: [0, 2, 1]}
+SERVE = {0: [3, 2, 1], 1: [0, 3, 2], 2: [3, 0, 1], 3: [2, 1, 0]}
+PIECES = {1: 2, 2: 1, 3: 1}
+
+
+def rank_program(g, core, T, topo):
+    rank = T.rank_of(core)
+    if rank is None:
+        return
+    vec, act, ten, sync = g.vector, g.scalar, g.tensor, g.sync
+    used = [0]
+
+    def ev(ins, n=1):
+        name = "e%d" % used[0]
+        used[0] += 1
+        ins.then_inc(T.sem[name], n)
+        return (name, n)
+
+    def wait(q, *evs):
+        for name, n in evs:
+            q.wait_ge(T.sem[name], n)
+
+    sent = [0]
+
+    def send(dst_rank, out_ap, in_ap, sem):
+        dst = T.cores[dst_rank]
+        rid, pid, _se = topo.addr(dst)
+        g.remote_dma(out_ap, in_ap, T.sem[sem], T.sem["ls"], pid, rid, topo.mask(core, dst))
+        sent[0] += len(topo.engines(core, dst))
+
+    def arrived(src_rank, sem):
+        return (sem, len(topo.engines(T.cores[src_rank], core)))
+
+    def slot(buf, r, w):
+        return buf[:, r * w:(r + 1) * w]
+
+    e_ids = ev(sync.dma_start(slot(T.idl, rank, L), T.ids[:]), 16)
+    e_hs = ev(act.dma_start(T.hsi[:], T.hs[:]), 16)
+    e_mat = ev(sync.dma_start(T.win[:], T.mat[:]), 16)
+
+    e_p = ev(g.iota(T.pidx[:], [[1, 1]], 0, 1))
+    e_km = ev(g.iota(T.km[:], [[1, 32], [0, 4]], 0, 0, allow_small_or_imprecise_dtypes=True))
+    e_m32 = ev(g.iota(T.m32[:], [[1, 32]], 0, 0, allow_small_or_imprecise_dtypes=True))
+    wait(g, e_ids)
+    for r in IDS_TO[rank]:
+        send(r, slot(T.idl, rank, L), slot(T.idl, rank, L), "ida%d" % rank)
+
+    wait(vec, e_p)
+    e1 = ev(vec.tensor_scalar(T.i1[:], T.pidx[:], 2, 28, A.logical_shift_right, A.bitwise_and))
+    e2 = ev(vec.tensor_scalar(T.i2[:], T.pidx[:], 3, None, A.bitwise_and))
+    wait(vec, e1, e2)
+    e_key = ev(vec.tensor_tensor(T.keyp[:], T.i1[:], T.i2[:], A.add))
+    if rank == 0:
+        e3 = ev(vec.tensor_scalar(T.i3[:], T.pidx[:], 12, None, A.bitwise_and))
+        wait(vec, e3, e_key)
+        e_k0 = ev(vec.tensor_scalar(T.key0[:], T.i3[:], 100.0, T.keyp[:, 0:1], A.mult, A.add))
+    else:
+        e_k0 = ev(vec.tensor_copy(T.key0[:], T.pidx[:]))
+        wait(vec, e_key)
+    wait(vec, e_km, e_m32)
+    e_sb = ev(vec.tensor_scalar(T.sb[:], T.km[:], T.keyp[:, 0:1], None, A.is_equal))
+    e_sf = ev(vec.tensor_scalar(T.sf[:], T.km[:], T.keyp[:, 0:1], None, A.is_equal))
+    e_so = ev(vec.tensor_scalar(T.so[:], T.m32[:], T.keyp[:, 0:1], None, A.is_equal))
+    wait(vec, e_k0)
+    consts = [e_sb, e_sf, e_so]
+    if rank == 0:
+        consts.append(ev(vec.tensor_scalar(T.ex[:, 0:128], T.km[:], T.key0[:, 0:1], None, A.is_equal)))
+        e_c = ev(vec.memset(T.cm[:], 0.0))
+        wait(vec, e_c)
+        for b in range(4):
+            o = 128 * b + 32 * b
+            consts.append(ev(vec.tensor_scalar(T.cm[:, o:o + 32], T.m32[:], T.key0[:, 0:1], None, A.is_equal)))
+    else:
+        for b in range(4):
+            consts.append(ev(vec.tensor_scalar(T.ex[:, 128 * b:128 * b + 128], T.km[:], float(32 * b), T.key0[:, 0:1],
+                                               A.add, A.is_equal)))
+    wait(ten, *consts)
+
+    wait(vec, e_hs)
+    e_hf = ev(vec.tensor_copy(T.hsf[:], T.hsi[:]))
+    wait(vec, e_hf)
+
+    gathered = {}
+
+    def hash_and_gather(r):
+        wait(vec, e_ids if r == rank else arrived(r, "ida%d" % r))
+        a = ev(vec.tensor_scalar(slot(T.t1, r, L), slot(T.idl, r, L), T.hsf[:, 0:1], T.hsf[:, 1:2], A.mult, A.add))
+        wait(vec, a)
+        b = ev(vec.tensor_scalar(slot(T.t2, r, L), slot(T.t1, r, L), 4, 4095, A.logical_shift_right, A.bitwise_and))
+        wait(vec, b)
+        c = ev(vec.tensor_copy(slot(T.offs, r, L), slot(T.t2, r, L)))
+        wait(vec, c)
+        wait(act, c)
+        if r == rank:
+            wait(vec, e_mat)
+            wait(act, e_mat)
+        o, m = r * L, r * K
+        gv = ev(vec.tensor_copy(T.gat[:, m:m + H], T.win[:].indirect(T.offs[:, o:o + L // 2])))
+        gs = ev(act.activation(T.gat[:, m + H:m + K], T.win[:].indirect(T.offs[:, o + L // 2:o + L]),
+                               ActivationFunctionType.Copy))
+        gathered[r] = [gv, gs]
+
+    hash_and_gather(rank)
+    V0 = [T.pv00, T.pv01]
+    V1 = [T.pv10, T.pv11]
+    V2 = [T.pv20, T.pv21]
+    e_v0 = [[], []]
+    if rank == 0:
+        for h in range(2):
+            wait(ten, gathered[0][h])
+            e_v0[h].append(ev(ten.matmul(V0[h][:], T.ex[:, 0:128], T.gat[:, h * H:(h + 1) * H], True, True)))
+        packs = [T.pv10, T.pv11, T.pv20]
+        copies = []
+
+        def pack(i, r):
+            wait(ten, *gathered[r])
+            ins = None
+            for b in range(4):
+                m = r * K + 256 * b
+                ins = ten.matmul(packs[i][:, 0:256], T.cm[:, 128 * b:128 * b + 128], T.gat[:, m:m + 256], b == 0, b == 3)
+            return ev(ins)
+
+        def unload(i, r, e):
+            wait(act, e)
+            e = ev(act.activation(slot(T.c0s, r, 256), packs[i][:, 0:256], ActivationFunctionType.Copy))
+            copies.append(e)
+            wait(g, e)
+            send(r, T.c0l[:], slot(T.c0s, r, 256), "va")
+
+        a, b, c = SERVE[0]
+        hash_and_gather(a)
+        ea = pack(0, a)
+        hash_and_gather(b)
+        unload(0, a, ea)
+        eb = pack(1, b)
+        hash_and_gather(c)
+        unload(1, b, eb)
+        ec = pack(2, c)
+        unload(2, c, ec)
+        wait(ten, *copies)
+    else:
+        for r in SERVE[rank]:
+            hash_and_gather(r)
+        n = PIECES[rank]
+        w = K // n
+        for p in range(n):
+            for r in SERVE[rank]:
+                wait(g, *(gathered[r] if n == 1 else [gathered[r][p]]))
+                m = r * K + p * w
+                q = rank * K + p * w
+                send(r, T.land[:, q:q + w], T.gat[:, m:m + w], "ma%d_%d" % (rank, p))
+        wait(ten, arrived(0, "va"))
+        for b in range(4):
+            h = b // 2
+            o = 256 * (b % 2)
+            e_v0[h].append(ev(ten.matmul(V0[h][:, o:o + 256], T.ex[:, 128 * b:128 * b + 128], T.c0l[:], True, True)))
+
+    def picks(s, h):
+        if s == rank:
+            m = rank * K + h * H
+            return T.gat[:, m:m + H], [gathered[rank][h]]
+        m = s * K + h * H
+        return T.land[:, m:m + H], [arrived(s, "ma%d_%d" % (s, h if PIECES[s] == 2 else 0))]
+
+    half = [slice(0, H), slice(H, K)]
+    P1 = [T.pp0, T.pp1]
+    e_hi, e_mm = {}, {}
+
+    def mult1(h):
+        ap, evs = picks(1, h)
+        wait(vec, *e_v0[h])
+        wait(vec, *evs)
+        e = ev(vec.tensor_tensor(P1[h][:], V0[h][:], ap, A.mult))
+        wait(act, e)
+        e_hi[h] = ev(act.activation(T.hi[:, half[h]], P1[h][:], ActivationFunctionType.Copy))
+
+    def step1(h):
+        wait(vec, e_hi[h])
+        e = ev(vec.tensor_tensor(T.lo[:, half[h]], P1[h][:], T.hi[:, half[h]], A.subtract))
+        wait(ten, e_hi[h])
+        ten.matmul(V1[h][:], T.sb[:], T.hi[:, half[h]], True, False)
+        wait(ten, e)
+        e_mm[1, h] = ev(ten.matmul(V1[h][:], T.sb[:], T.lo[:, half[h]], False, True))
+
+    def step2(h):
+        ap, evs = picks(2, h)
+        wait(vec, e_mm[1, h])
+        wait(vec, *evs)
+        e = ev(vec.tensor_tensor(T.p2[:, half[h]], V1[h][:], ap, A.mult))
+        wait(ten, e)
+        e_mm[2, h] = ev(ten.matmul(V2[h][:], T.sf[:], T.p2[:, half[h]], True, True))
+
+    def step3(h):
+        ap, evs = picks(3, h)
+        wait(vec, e_mm[2, h])
+        wait(vec, *evs)
+        e = ev(vec.tensor_tensor(T.p3[:, half[h]], V2[h][:], ap, A.mult))
+        wait(ten, e)
+        e_mm[3, h] = ev(ten.matmul(V0[h][0:32, :], T.so[:], T.p3[:, half[h]], True, True))
+
+    if rank == 1:
+        mult1(0), mult1(1), step1(0), step1(1), step2(0), step2(1), step3(0), step3(1)
+    else:
+        mult1(0), step1(0), step2(0), mult1(1), step1(1), step3(0), step2(1), step3(1)
+
+    wait(act, e_mm[3, 0])
+    ey0 = ev(act.activation(T.yb[0:32, half[0]], V0[0][0:32, :], ActivationFunctionType.Copy))
+    wait(vec, e_mm[3, 1])
+    ey1 = ev(vec.tensor_copy(T.yb[0:32, half[1]], V0[1][0:32, :]))
+    wait(sync, ey0)
+    d0 = ev(sync.dma_start(T.y[:, half[0]], T.yb[0:32, half[0]]), 16)
+    wait(sync, ey1)
+    d1 = ev(sync.dma_start(T.y[:, half[1]], T.yb[0:32, half[1]]), 16)
+    wait(sync, d0, d1)
+    wait(g, ("ls", sent[0]))

@@ -2,7 +2,8 @@ from concourse.mybir import AluOpType, ActivationFunctionType
 
 N = 4
 K = 1024
-H = K // 2
+C = 256
+NC = K // C
 L = K // 16
 A = AluOpType
 
@@ -36,21 +37,23 @@ SCRATCH = {
     "so": ("sbuf", [128, 32], "float32"),
     "ex": ("sbuf", [128, 512], "bfloat16"),
     "cm": ("sbuf", [128, 512], "bfloat16"),
-    "pv00": ("psum", [128, H], "float32"),
-    "pv01": ("psum", [128, H], "float32"),
-    "pv10": ("psum", [128, H], "float32"),
-    "pv11": ("psum", [128, H], "float32"),
-    "pv20": ("psum", [128, H], "float32"),
-    "pv21": ("psum", [128, H], "float32"),
-    "pp0": ("psum", [128, H], "float32"),
-    "pp1": ("psum", [128, H], "float32"),
 }
-SEMAPHORES = (["e%d" % i for i in range(100)] + ["ida%d" % r for r in range(N)]
+for _b in range(NC):
+    SCRATCH["pa%d" % _b] = ("psum", [128, 2 * C], "float32")
+    SCRATCH["pb%d" % _b] = ("psum", [128, 2 * C], "float32")
+SEMAPHORES = (["e%d" % i for i in range(120)] + ["ida%d" % r for r in range(N)]
               + ["ma%d_%d" % (q, h) for q in range(1, N) for h in range(2)] + ["va", "ls"])
 
-IDS_TO = {0: [1, 2, 3], 1: [0, 3, 2], 2: [3, 0, 1], 3: [0, 2, 1]}
-SERVE = {0: [3, 2, 1], 1: [0, 3, 2], 2: [3, 0, 1], 3: [2, 1, 0]}
+IDS_TO = {0: [3, 2, 1], 1: [0, 3, 2], 2: [1, 3, 0], 3: [1, 0, 2]}
+SERVE = {0: [1, 3, 2], 1: [2, 3, 0], 2: [0, 1, 3], 3: [2, 1, 0]}
 PIECES = {1: 2, 2: 1, 3: 1}
+HALF = (("v", 0, 2), ("s", 2, 4))
+SPLIT = {0: (("v", 0, 1), ("s", 1, 3), ("s", 3, 4)), 1: (("v", 0, 1), ("s", 1, 2), ("v", 2, 3), ("s", 3, 4)),
+         2: HALF, 3: HALF}
+ORDER = {0: "m10 m11 lo0 lo1 m20 m21 m30 m12 m13 lo2 m31 lo3 m22 m23 m32 m33",
+         1: "m10 m11 m12 lo0 lo1 lo2 m20 m13 m22 m21 lo3 m30 m31 m23 m32 m33",
+         2: "m10 m11 m12 lo0 lo1 lo2 m20 m22 m13 m21 lo3 m30 m23 m31 m32 m33",
+         3: "m10 m11 lo0 lo1 m12 m20 m13 lo2 m21 m30 lo3 m22 m31 m23 m32 m33"}
 
 
 def rank_program(g, core, T, topo):
@@ -144,49 +147,45 @@ def rank_program(g, core, T, topo):
         if r == rank:
             wait(vec, e_mat)
             wait(act, e_mat)
-        o, m = r * L, r * K
-        gv = ev(vec.tensor_copy(T.gat[:, m:m + H], T.win[:].indirect(T.offs[:, o:o + L // 2])))
-        gs = ev(act.activation(T.gat[:, m + H:m + K], T.win[:].indirect(T.offs[:, o + L // 2:o + L]),
-                               ActivationFunctionType.Copy))
-        gathered[r] = [gv, gs]
+        gathered[r] = {}
+        for q, b0, b1 in HALF if r == rank else SPLIT[rank]:
+            dst = T.gat[:, r * K + b0 * C:r * K + b1 * C]
+            src = T.win[:].indirect(T.offs[:, r * L + b0 * C // 16:r * L + b1 * C // 16])
+            e = ev(vec.tensor_copy(dst, src) if q == "v" else act.activation(dst, src, ActivationFunctionType.Copy))
+            for b in range(b0, b1):
+                gathered[r][b] = e
 
     hash_and_gather(rank)
-    V0 = [T.pv00, T.pv01]
-    V1 = [T.pv10, T.pv11]
-    V2 = [T.pv20, T.pv21]
-    e_v0 = [[], []]
+    PA = [T["pa%d" % b] for b in range(NC)]
+    PB = [T["pb%d" % b] for b in range(NC)]
+    left, right = slice(0, C), slice(C, 2 * C)
+    col = [slice(b * C, (b + 1) * C) for b in range(NC)]
+    e_v0 = {}
     if rank == 0:
-        for h in range(2):
-            wait(ten, gathered[0][h])
-            e_v0[h].append(ev(ten.matmul(V0[h][:], T.ex[:, 0:128], T.gat[:, h * H:(h + 1) * H], True, True)))
-        packs = [T.pv10, T.pv11, T.pv20]
-        copies = []
+        for b in range(NC):
+            wait(ten, gathered[0][b])
+            e_v0[b] = ev(ten.matmul(PA[b][:, left], T.ex[:, 0:128], T.gat[:, col[b]], True, True))
+        copies, packed = [], []
 
-        def pack(i, r):
-            wait(ten, *gathered[r])
-            ins = None
-            for b in range(4):
-                m = r * K + 256 * b
-                ins = ten.matmul(packs[i][:, 0:256], T.cm[:, 128 * b:128 * b + 128], T.gat[:, m:m + 256], b == 0, b == 3)
-            return ev(ins)
-
-        def unload(i, r, e):
-            wait(act, e)
-            e = ev(act.activation(slot(T.c0s, r, 256), packs[i][:, 0:256], ActivationFunctionType.Copy))
+        def unload(i):
+            r = SERVE[0][i]
+            wait(vec, packed[i])
+            e = ev(vec.tensor_copy(slot(T.c0s, r, 256), PB[i][:, 0:256]))
             copies.append(e)
             wait(g, e)
             send(r, T.c0l[:], slot(T.c0s, r, 256), "va")
 
-        a, b, c = SERVE[0]
-        hash_and_gather(a)
-        ea = pack(0, a)
-        hash_and_gather(b)
-        unload(0, a, ea)
-        eb = pack(1, b)
-        hash_and_gather(c)
-        unload(1, b, eb)
-        ec = pack(2, c)
-        unload(2, c, ec)
+        for i, r in enumerate(SERVE[0]):
+            hash_and_gather(r)
+            ins = None
+            for b in range(NC):
+                wait(ten, gathered[r][b])
+                m = r * K + b * C
+                ins = ten.matmul(PB[i][:, 0:256], T.cm[:, 128 * b:128 * b + 128], T.gat[:, m:m + C], b == 0, b == NC - 1)
+            packed.append(ev(ins))
+            if i:
+                unload(i - 1)
+        unload(N - 2)
         wait(ten, *copies)
     else:
         for r in SERVE[rank]:
@@ -195,71 +194,64 @@ def rank_program(g, core, T, topo):
         w = K // n
         for p in range(n):
             for r in SERVE[rank]:
-                wait(g, *(gathered[r] if n == 1 else [gathered[r][p]]))
+                wait(g, *sorted(set(gathered[r][b] for b in range(p * NC // n, (p + 1) * NC // n))))
                 m = r * K + p * w
                 q = rank * K + p * w
                 send(r, T.land[:, q:q + w], T.gat[:, m:m + w], "ma%d_%d" % (rank, p))
         wait(ten, arrived(0, "va"))
-        for b in range(4):
-            h = b // 2
-            o = 256 * (b % 2)
-            e_v0[h].append(ev(ten.matmul(V0[h][:, o:o + 256], T.ex[:, 128 * b:128 * b + 128], T.c0l[:], True, True)))
+        for b in range(NC):
+            e_v0[b] = ev(ten.matmul(PA[b][:, left], T.ex[:, 128 * b:128 * b + 128], T.c0l[:], True, True))
 
-    def picks(s, h):
+    def picks(s, b):
+        m = s * K + b * C
         if s == rank:
-            m = rank * K + h * H
-            return T.gat[:, m:m + H], [gathered[rank][h]]
-        m = s * K + h * H
-        return T.land[:, m:m + H], [arrived(s, "ma%d_%d" % (s, h if PIECES[s] == 2 else 0))]
+            return T.gat[:, m:m + C], gathered[rank][b]
+        return T.land[:, m:m + C], arrived(s, "ma%d_%d" % (s, b // 2 if PIECES[s] == 2 else 0))
 
-    half = [slice(0, H), slice(H, K)]
-    P1 = [T.pp0, T.pp1]
     e_hi, e_mm = {}, {}
 
-    def mult1(h):
-        ap, evs = picks(1, h)
-        wait(vec, *e_v0[h])
-        wait(vec, *evs)
-        e = ev(vec.tensor_tensor(P1[h][:], V0[h][:], ap, A.mult))
+    def m1(b):
+        ap, e = picks(1, b)
+        wait(vec, e_v0[b], e)
+        e = ev(vec.tensor_tensor(PA[b][:, right], PA[b][:, left], ap, A.mult))
         wait(act, e)
-        e_hi[h] = ev(act.activation(T.hi[:, half[h]], P1[h][:], ActivationFunctionType.Copy))
+        e_hi[b] = ev(act.activation(T.hi[:, col[b]], PA[b][:, right], ActivationFunctionType.Copy))
 
-    def step1(h):
-        wait(vec, e_hi[h])
-        e = ev(vec.tensor_tensor(T.lo[:, half[h]], P1[h][:], T.hi[:, half[h]], A.subtract))
-        wait(ten, e_hi[h])
-        ten.matmul(V1[h][:], T.sb[:], T.hi[:, half[h]], True, False)
+    def lo(b):
+        wait(vec, e_hi[b])
+        e = ev(vec.tensor_tensor(T.lo[:, col[b]], PA[b][:, right], T.hi[:, col[b]], A.subtract))
+        wait(ten, e_hi[b])
+        ten.matmul(PB[b][:, left], T.sb[:], T.hi[:, col[b]], True, False)
         wait(ten, e)
-        e_mm[1, h] = ev(ten.matmul(V1[h][:], T.sb[:], T.lo[:, half[h]], False, True))
+        e_mm[1, b] = ev(ten.matmul(PB[b][:, left], T.sb[:], T.lo[:, col[b]], False, True))
 
-    def step2(h):
-        ap, evs = picks(2, h)
-        wait(vec, e_mm[1, h])
-        wait(vec, *evs)
-        e = ev(vec.tensor_tensor(T.p2[:, half[h]], V1[h][:], ap, A.mult))
+    def m2(b):
+        ap, e = picks(2, b)
+        wait(vec, e_mm[1, b], e)
+        e = ev(vec.tensor_tensor(T.p2[:, col[b]], PB[b][:, left], ap, A.mult))
         wait(ten, e)
-        e_mm[2, h] = ev(ten.matmul(V2[h][:], T.sf[:], T.p2[:, half[h]], True, True))
+        e_mm[2, b] = ev(ten.matmul(PB[b][:, right], T.sf[:], T.p2[:, col[b]], True, True))
 
-    def step3(h):
-        ap, evs = picks(3, h)
-        wait(vec, e_mm[2, h])
-        wait(vec, *evs)
-        e = ev(vec.tensor_tensor(T.p3[:, half[h]], V2[h][:], ap, A.mult))
+    def m3(b):
+        ap, e = picks(3, b)
+        wait(vec, e_mm[2, b], e)
+        e = ev(vec.tensor_tensor(T.p3[:, col[b]], PB[b][:, right], ap, A.mult))
         wait(ten, e)
-        e_mm[3, h] = ev(ten.matmul(V0[h][0:32, :], T.so[:], T.p3[:, half[h]], True, True))
+        e_mm[3, b] = ev(ten.matmul(PA[b][0:32, left], T.so[:], T.p3[:, col[b]], True, True))
 
-    if rank == 1:
-        mult1(0), mult1(1), step1(0), step1(1), step2(0), step2(1), step3(0), step3(1)
-    else:
-        mult1(0), step1(0), step2(0), mult1(1), step1(1), step3(0), step2(1), step3(1)
+    do = {"m1": m1, "lo": lo, "m2": m2, "m3": m3}
+    for step in ORDER[rank].split():
+        do[step[:2]](int(step[2]))
 
-    wait(act, e_mm[3, 0])
-    ey0 = ev(act.activation(T.yb[0:32, half[0]], V0[0][0:32, :], ActivationFunctionType.Copy))
-    wait(vec, e_mm[3, 1])
-    ey1 = ev(vec.tensor_copy(T.yb[0:32, half[1]], V0[1][0:32, :]))
-    wait(sync, ey0)
-    d0 = ev(sync.dma_start(T.y[:, half[0]], T.yb[0:32, half[0]]), 16)
-    wait(sync, ey1)
-    d1 = ev(sync.dma_start(T.y[:, half[1]], T.yb[0:32, half[1]]), 16)
-    wait(sync, d0, d1)
+    stored = []
+    for b in range(NC):
+        q = vec if b == NC - 1 else act
+        wait(q, e_mm[3, b])
+        if q is vec:
+            e = ev(vec.tensor_copy(T.yb[0:32, col[b]], PA[b][0:32, left]))
+        else:
+            e = ev(act.activation(T.yb[0:32, col[b]], PA[b][0:32, left], ActivationFunctionType.Copy))
+        wait(sync, e)
+        stored.append(ev(sync.dma_start(T.y[:, col[b]], T.yb[0:32, col[b]]), 16))
+    wait(sync, *stored)
     wait(g, ("ls", sent[0]))

@@ -21,9 +21,10 @@ SCRATCH = {
     "c0l": ("sbuf", [128, 256], "bfloat16"),
     "hi": ("sbuf", [128, K], "bfloat16"),
     "lo": ("sbuf", [128, K], "bfloat16"),
+    "p1": ("sbuf", [128, K], "float32"),
     "p2": ("sbuf", [128, K], "float32"),
     "p3": ("sbuf", [128, K], "float32"),
-    "yb": ("sbuf", [128, K], "float32"),
+    "yb": ("sbuf", [128, NC * 64], "float32"),
     "km": ("sbuf", [128, 128], "float32"),
     "m32": ("sbuf", [128, 32], "float32"),
     "pidx": ("sbuf", [128, 1], "int32"),
@@ -41,24 +42,56 @@ SCRATCH = {
 for _b in range(NC):
     SCRATCH["pa%d" % _b] = ("psum", [128, 2 * C], "float32")
     SCRATCH["pb%d" % _b] = ("psum", [128, 2 * C], "float32")
-SEMAPHORES = (["e%d" % i for i in range(120)] + ["ida%d" % r for r in range(N)]
-              + ["ma%d_%d" % (q, h) for q in range(1, N) for h in range(2)] + ["va", "ls"])
+SEMAPHORES = (["e%d" % i for i in range(118)] + ["ida%d" % r for r in range(N)]
+              + ["ma%d_%d" % (q, b) for q in range(1, N) for b in range(NC)]
+              + ["rl%d" % i for i in range(10)] + ["va", "ls", "st"])
 
-IDS_TO = {0: [3, 2, 1], 1: [0, 3, 2], 2: [1, 3, 0], 3: [1, 0, 2]}
+IDS_TO = {0: [2, 1, 3], 1: [0, 3, 2], 2: [1, 0, 3], 3: [0, 1, 2]}
 SERVE = {0: [1, 3, 2], 1: [2, 3, 0], 2: [0, 1, 3], 3: [2, 1, 0]}
-PIECES = {1: 2, 2: 1, 3: 1}
+PLAN = {1: [(2, 0, 3, -1), (2, 3, 4, 0), (3, 0, 3, -1), (3, 3, 4, 1), (0, 0, 3, -1), (0, 3, 4, 0)],
+        2: [(0, 0, 2, -1), (0, 2, 3, -1), (1, 3, 4, 1), (0, 3, 4, 0), (1, 0, 3, -1), (3, 0, 3, -1), (3, 3, 4, 0)],
+        3: [(2, 0, 3, -1), (2, 3, 4, 0), (1, 0, 3, -1), (1, 3, 4, 1), (0, 0, 2, -1), (0, 2, 3, 0), (0, 3, 4, 0)]}
 HALF = (("v", 0, 2), ("s", 2, 4))
 SPLIT = {0: (("v", 0, 1), ("s", 1, 3), ("s", 3, 4)), 1: (("v", 0, 1), ("s", 1, 2), ("v", 2, 3), ("s", 3, 4)),
-         2: HALF, 3: HALF}
-ORDER = {0: "m10 m11 lo0 lo1 m20 m21 m30 m12 m13 lo2 m31 lo3 m22 m23 m32 m33",
-         1: "m10 m11 m12 lo0 lo1 lo2 m20 m13 m22 m21 lo3 m30 m31 m23 m32 m33",
-         2: "m10 m11 m12 lo0 lo1 lo2 m20 m22 m13 m21 lo3 m30 m23 m31 m32 m33",
-         3: "m10 m11 lo0 lo1 m12 m20 m13 lo2 m21 m30 lo3 m22 m31 m23 m32 m33"}
+         2: (("v", 0, 1), ("v", 1, 2), ("s", 2, 3), ("s", 3, 4)), 3: (("v", 3, 4), ("s", 0, 1), ("s", 1, 3))}
+WHOLE = {0: (0,), 1: (0, 1), 2: (0,), 3: (0, 2)}
+ORDER = {0: "m10 m11 lo1 m20 m21 m12 m13 lo2 m30 lo3 m31 m22 ou0 m23 ou1 m32 m33 ou2 ou3",
+         1: "m10 m11 m12 m13 lo2 lo3 m21 m22 m20 m23 m30 m31 ou0 m32 ou1 m33 ou2 ou3",
+         2: "m10 m11 m12 lo1 m20 m13 lo2 m21 lo3 m22 m30 m23 m31 ou0 m32 m33 ou1 ou2 ou3",
+         3: "m10 m11 m12 m20 lo1 m13 m30 m21 lo3 m22 m31 ou0 m23 ou1 m32 m33 ou2 ou3"}
+
+
+def relays_of(core, T, topo):
+    c = [x for x in topo.cores_of(core) if x != core and all(topo.may_write(x, d) for d in T.cores)]
+    return [x for x in c if topo.die(x) != topo.die(core)] + [x for x in c if topo.die(x) == topo.die(core)]
+
+
+def inner_engines(core, relay, dst, topo):
+    return [e for e in topo.engines(core, relay) if e not in topo.engines(core, dst)]
+
+
+def relay_program(g, core, q, way, T, topo):
+    sent = 0
+    for i, (r, c0, c1, w) in enumerate(PLAN[q]):
+        if w != way:
+            continue
+        dst = T.cores[r]
+        rid, pid, _se = topo.addr(dst)
+        g.wait_ge(T.sem["rl%d" % i], len(inner_engines(T.cores[q], core, dst, topo)))
+        g.remote_dma(T.land[:, q * K + c0 * C:q * K + c1 * C], T.gat[:, r * K + c0 * C:r * K + c1 * C],
+                     T.sem["ma%d_%d" % (q, c0)], T.sem["ls"], pid, rid, topo.mask(core, dst))
+        sent += len(topo.engines(core, dst))
+    if sent:
+        g.wait_ge(T.sem["ls"], sent)
 
 
 def rank_program(g, core, T, topo):
     rank = T.rank_of(core)
     if rank is None:
+        for q in PLAN:
+            relays = relays_of(T.cores[q], T, topo)
+            if core in relays:
+                relay_program(g, core, q, relays.index(core), T, topo)
         return
     vec, act, ten, sync = g.vector, g.scalar, g.tensor, g.sync
     used = [0]
@@ -135,7 +168,7 @@ def rank_program(g, core, T, topo):
 
     gathered = {}
 
-    def hash_and_gather(r):
+    def hash_list(r):
         wait(vec, e_ids if r == rank else arrived(r, "ida%d" % r))
         a = ev(vec.tensor_scalar(slot(T.t1, r, L), slot(T.idl, r, L), T.hsf[:, 0:1], T.hsf[:, 1:2], A.mult, A.add))
         wait(vec, a)
@@ -147,15 +180,18 @@ def rank_program(g, core, T, topo):
         if r == rank:
             wait(vec, e_mat)
             wait(act, e_mat)
+
+    def gather(r, split):
         gathered[r] = {}
-        for q, b0, b1 in HALF if r == rank else SPLIT[rank]:
+        for q, b0, b1 in split:
             dst = T.gat[:, r * K + b0 * C:r * K + b1 * C]
             src = T.win[:].indirect(T.offs[:, r * L + b0 * C // 16:r * L + b1 * C // 16])
             e = ev(vec.tensor_copy(dst, src) if q == "v" else act.activation(dst, src, ActivationFunctionType.Copy))
             for b in range(b0, b1):
                 gathered[r][b] = e
 
-    hash_and_gather(rank)
+    hash_list(rank)
+    gather(rank, HALF)
     PA = [T["pa%d" % b] for b in range(NC)]
     PB = [T["pb%d" % b] for b in range(NC)]
     left, right = slice(0, C), slice(C, 2 * C)
@@ -176,7 +212,8 @@ def rank_program(g, core, T, topo):
             send(r, T.c0l[:], slot(T.c0s, r, 256), "va")
 
         for i, r in enumerate(SERVE[0]):
-            hash_and_gather(r)
+            hash_list(r)
+            gather(r, SPLIT[0])
             ins = None
             for b in range(NC):
                 wait(ten, gathered[r][b])
@@ -189,33 +226,50 @@ def rank_program(g, core, T, topo):
         wait(ten, *copies)
     else:
         for r in SERVE[rank]:
-            hash_and_gather(r)
-        n = PIECES[rank]
-        w = K // n
-        for p in range(n):
-            for r in SERVE[rank]:
-                wait(g, *sorted(set(gathered[r][b] for b in range(p * NC // n, (p + 1) * NC // n))))
-                m = r * K + p * w
-                q = rank * K + p * w
-                send(r, T.land[:, q:q + w], T.gat[:, m:m + w], "ma%d_%d" % (rank, p))
+            hash_list(r)
+            gather(r, SPLIT[rank])
+        relays = relays_of(core, T, topo)
+        for i, (r, c0, c1, way) in enumerate(PLAN[rank]):
+            wait(g, *sorted(set(gathered[r][b] for b in range(c0, c1))))
+            m = slice(r * K + c0 * C, r * K + c1 * C)
+            if way < 0:
+                send(r, T.land[:, rank * K + c0 * C:rank * K + c1 * C], T.gat[:, m], "ma%d_%d" % (rank, c0))
+            else:
+                rid, pid, _se = topo.addr(relays[way])
+                eng = inner_engines(core, relays[way], T.cores[r], topo)
+                g.remote_dma(T.gat[:, m], T.gat[:, m], T.sem["rl%d" % i], T.sem["ls"], pid, rid, sum(1 << e for e in eng))
+                sent[0] += len(eng)
         wait(ten, arrived(0, "va"))
         for b in range(NC):
             e_v0[b] = ev(ten.matmul(PA[b][:, left], T.ex[:, 128 * b:128 * b + 128], T.c0l[:], True, True))
+
+    came = {}
+    for q in PLAN:
+        for r, c0, c1, way in PLAN[q]:
+            if r == rank:
+                src = T.cores[q] if way < 0 else relays_of(T.cores[q], T, topo)[way]
+                for b in range(c0, c1):
+                    came[q, b] = ("ma%d_%d" % (q, c0), len(topo.engines(src, core)))
 
     def picks(s, b):
         m = s * K + b * C
         if s == rank:
             return T.gat[:, m:m + C], gathered[rank][b]
-        return T.land[:, m:m + C], arrived(s, "ma%d_%d" % (s, b // 2 if PIECES[s] == 2 else 0))
+        return T.land[:, m:m + C], came[s, b]
 
-    e_hi, e_mm = {}, {}
+    e_hi, e_mm, e_fin = {}, {}, {}
 
     def m1(b):
         ap, e = picks(1, b)
         wait(vec, e_v0[b], e)
-        e = ev(vec.tensor_tensor(PA[b][:, right], PA[b][:, left], ap, A.mult))
-        wait(act, e)
-        e_hi[b] = ev(act.activation(T.hi[:, col[b]], PA[b][:, right], ActivationFunctionType.Copy))
+        if b in WHOLE[rank]:
+            e = ev(vec.tensor_tensor(T.p1[:, col[b]], PA[b][:, left], ap, A.mult))
+            wait(ten, e)
+            e_mm[1, b] = ev(ten.matmul(PB[b][:, left], T.sf[:], T.p1[:, col[b]], True, True))
+        else:
+            e = ev(vec.tensor_tensor(PA[b][:, right], PA[b][:, left], ap, A.mult))
+            wait(act, e)
+            e_hi[b] = ev(act.activation(T.hi[:, col[b]], PA[b][:, right], ActivationFunctionType.Copy))
 
     def lo(b):
         wait(vec, e_hi[b])
@@ -237,21 +291,25 @@ def rank_program(g, core, T, topo):
         wait(vec, e_mm[2, b], e)
         e = ev(vec.tensor_tensor(T.p3[:, col[b]], PB[b][:, right], ap, A.mult))
         wait(ten, e)
-        e_mm[3, b] = ev(ten.matmul(PA[b][0:32, left], T.so[:], T.p3[:, col[b]], True, True))
-
-    do = {"m1": m1, "lo": lo, "m2": m2, "m3": m3}
-    for step in ORDER[rank].split():
-        do[step[:2]](int(step[2]))
+        e_fin[b] = [ev(ten.matmul(PA[b][:, 32 * j:32 * j + 32], T.p3[:, b * C + j:(b + 1) * C:2], T.so[:], True, True))
+                    for j in range(2)]
 
     stored = []
-    for b in range(NC):
-        q = vec if b == NC - 1 else act
-        wait(q, e_mm[3, b])
-        if q is vec:
-            e = ev(vec.tensor_copy(T.yb[0:32, col[b]], PA[b][0:32, left]))
-        else:
-            e = ev(act.activation(T.yb[0:32, col[b]], PA[b][0:32, left], ActivationFunctionType.Copy))
-        wait(sync, e)
-        stored.append(ev(sync.dma_start(T.y[:, col[b]], T.yb[0:32, col[b]]), 16))
-    wait(sync, *stored)
+
+    def out(b):
+        wait(vec, *e_fin[b])
+        for j in range(2):
+            e = ev(vec.transpose(T.yb[:, 64 * b + j:64 * b + 64:2], PA[b][:, 32 * j:32 * j + 32]))
+            wait(sync, e)
+            wait(act, e)
+        for a in range(4):
+            q = act if a % 2 else sync
+            o = b * C + 64 * a
+            q.dma_start(T.y[:, o:o + 64], T.yb[32 * a:32 * a + 32, 64 * b:64 * b + 64]).then_inc(T.sem["st"], 16)
+            stored.append(16)
+
+    do = {"m1": m1, "lo": lo, "m2": m2, "m3": m3, "ou": out}
+    for step in ORDER[rank].split():
+        do[step[:2]](int(step[2]))
+    wait(sync, ("st", sum(stored)))
     wait(g, ("ls", sent[0]))

from concourse.mybir import AluOpType, ActivationFunctionType

N = 4
K = 1024
C = 256
NC = K // C
L = K // 16
A = AluOpType

SCRATCH = {
    "idl": ("sbuf", [128, N * L], "int32"),
    "hsi": ("sbuf", [128, 2], "int32"),
    "hsf": ("sbuf", [128, 2], "float32"),
    "win": ("sbuf", [128, 4096], "bfloat16"),
    "t1": ("sbuf", [128, N * L], "int32"),
    "t2": ("sbuf", [128, N * L], "int32"),
    "offs": ("sbuf", [128, N * L], "uint16"),
    "gat": ("sbuf", [128, N * K], "bfloat16"),
    "land": ("sbuf", [128, N * K], "bfloat16"),
    "c0s": ("sbuf", [128, N * 256], "bfloat16"),
    "c0l": ("sbuf", [128, 256], "bfloat16"),
    "hi": ("sbuf", [128, K], "bfloat16"),
    "lo": ("sbuf", [128, K], "bfloat16"),
    "p1": ("sbuf", [128, K], "float32"),
    "p2": ("sbuf", [128, K], "float32"),
    "p3": ("sbuf", [128, K], "float32"),
    "yb": ("sbuf", [128, NC * 64], "float32"),
    "km": ("sbuf", [128, 128], "float32"),
    "m32": ("sbuf", [128, 32], "float32"),
    "pidx": ("sbuf", [128, 1], "int32"),
    "i1": ("sbuf", [128, 1], "int32"),
    "i2": ("sbuf", [128, 1], "int32"),
    "i3": ("sbuf", [128, 1], "int32"),
    "keyp": ("sbuf", [128, 1], "float32"),
    "key0": ("sbuf", [128, 1], "float32"),
    "sf": ("sbuf", [128, 128], "float32"),
    "sb": ("sbuf", [128, 128], "bfloat16"),
    "so": ("sbuf", [128, 32], "float32"),
    "ex": ("sbuf", [128, 512], "bfloat16"),
    "cm": ("sbuf", [128, 512], "bfloat16"),
}
for _b in range(NC):
    SCRATCH["pa%d" % _b] = ("psum", [128, 2 * C], "float32")
    SCRATCH["pb%d" % _b] = ("psum", [128, 2 * C], "float32")
SEMAPHORES = (["e%d" % i for i in range(118)] + ["ida%d" % r for r in range(N)]
              + ["ma%d_%d" % (q, b) for q in range(1, N) for b in range(NC)]
              + ["rl%d" % i for i in range(10)] + ["va", "ls", "st"])

IDS_TO = {0: [2, 1, 3], 1: [0, 3, 2], 2: [1, 0, 3], 3: [0, 1, 2]}
SERVE = {0: [1, 3, 2], 1: [2, 3, 0], 2: [0, 1, 3], 3: [2, 1, 0]}
PLAN = {1: [(2, 0, 3, -1), (2, 3, 4, 0), (3, 0, 3, -1), (3, 3, 4, 1), (0, 0, 3, -1), (0, 3, 4, 0)],
        2: [(0, 0, 2, -1), (0, 2, 3, -1), (1, 3, 4, 1), (0, 3, 4, 0), (1, 0, 3, -1), (3, 0, 3, -1), (3, 3, 4, 0)],
        3: [(2, 0, 3, -1), (2, 3, 4, 0), (1, 0, 3, -1), (1, 3, 4, 1), (0, 0, 2, -1), (0, 2, 3, 0), (0, 3, 4, 0)]}
HALF = (("v", 0, 2), ("s", 2, 4))
SPLIT = {0: (("v", 0, 1), ("s", 1, 3), ("s", 3, 4)), 1: (("v", 0, 1), ("s", 1, 2), ("v", 2, 3), ("s", 3, 4)),
         2: (("v", 0, 1), ("v", 1, 2), ("s", 2, 3), ("s", 3, 4)), 3: (("v", 3, 4), ("s", 0, 1), ("s", 1, 3))}
WHOLE = {0: (0,), 1: (0, 1), 2: (0,), 3: (0, 2)}
ORDER = {0: "m10 m11 lo1 m20 m21 m12 m13 lo2 m30 lo3 m31 m22 ou0 m23 ou1 m32 m33 ou2 ou3",
         1: "m10 m11 m12 m13 lo2 lo3 m21 m22 m20 m23 m30 m31 ou0 m32 ou1 m33 ou2 ou3",
         2: "m10 m11 m12 lo1 m20 m13 lo2 m21 lo3 m22 m30 m23 m31 ou0 m32 m33 ou1 ou2 ou3",
         3: "m10 m11 m12 m20 lo1 m13 m30 m21 lo3 m22 m31 ou0 m23 ou1 m32 m33 ou2 ou3"}


def relays_of(core, T, topo):
    c = [x for x in topo.cores_of(core) if x != core and all(topo.may_write(x, d) for d in T.cores)]
    return [x for x in c if topo.die(x) != topo.die(core)] + [x for x in c if topo.die(x) == topo.die(core)]


def inner_engines(core, relay, dst, topo):
    return [e for e in topo.engines(core, relay) if e not in topo.engines(core, dst)]


def relay_program(g, core, q, way, T, topo):
    sent = 0
    for i, (r, c0, c1, w) in enumerate(PLAN[q]):
        if w != way:
            continue
        dst = T.cores[r]
        rid, pid, _se = topo.addr(dst)
        g.wait_ge(T.sem["rl%d" % i], len(inner_engines(T.cores[q], core, dst, topo)))
        g.remote_dma(T.land[:, q * K + c0 * C:q * K + c1 * C], T.gat[:, r * K + c0 * C:r * K + c1 * C],
                     T.sem["ma%d_%d" % (q, c0)], T.sem["ls"], pid, rid, topo.mask(core, dst))
        sent += len(topo.engines(core, dst))
    if sent:
        g.wait_ge(T.sem["ls"], sent)


def rank_program(g, core, T, topo):
    rank = T.rank_of(core)
    if rank is None:
        for q in PLAN:
            relays = relays_of(T.cores[q], T, topo)
            if core in relays:
                relay_program(g, core, q, relays.index(core), T, topo)
        return
    vec, act, ten, sync = g.vector, g.scalar, g.tensor, g.sync
    used = [0]

    def ev(ins, n=1):
        name = "e%d" % used[0]
        used[0] += 1
        ins.then_inc(T.sem[name], n)
        return (name, n)

    def wait(q, *evs):
        for name, n in evs:
            q.wait_ge(T.sem[name], n)

    sent = [0]

    def send(dst_rank, out_ap, in_ap, sem):
        dst = T.cores[dst_rank]
        rid, pid, _se = topo.addr(dst)
        g.remote_dma(out_ap, in_ap, T.sem[sem], T.sem["ls"], pid, rid, topo.mask(core, dst))
        sent[0] += len(topo.engines(core, dst))

    def arrived(src_rank, sem):
        return (sem, len(topo.engines(T.cores[src_rank], core)))

    def slot(buf, r, w):
        return buf[:, r * w:(r + 1) * w]

    e_ids = ev(sync.dma_start(slot(T.idl, rank, L), T.ids[:]), 16)
    e_hs = ev(act.dma_start(T.hsi[:], T.hs[:]), 16)
    e_mat = ev(sync.dma_start(T.win[:], T.mat[:]), 16)

    e_p = ev(g.iota(T.pidx[:], [[1, 1]], 0, 1))
    e_km = ev(g.iota(T.km[:], [[1, 32], [0, 4]], 0, 0, allow_small_or_imprecise_dtypes=True))
    e_m32 = ev(g.iota(T.m32[:], [[1, 32]], 0, 0, allow_small_or_imprecise_dtypes=True))
    wait(g, e_ids)
    for r in IDS_TO[rank]:
        send(r, slot(T.idl, rank, L), slot(T.idl, rank, L), "ida%d" % rank)

    wait(vec, e_p)
    e1 = ev(vec.tensor_scalar(T.i1[:], T.pidx[:], 2, 28, A.logical_shift_right, A.bitwise_and))
    e2 = ev(vec.tensor_scalar(T.i2[:], T.pidx[:], 3, None, A.bitwise_and))
    wait(vec, e1, e2)
    e_key = ev(vec.tensor_tensor(T.keyp[:], T.i1[:], T.i2[:], A.add))
    if rank == 0:
        e3 = ev(vec.tensor_scalar(T.i3[:], T.pidx[:], 12, None, A.bitwise_and))
        wait(vec, e3, e_key)
        e_k0 = ev(vec.tensor_scalar(T.key0[:], T.i3[:], 100.0, T.keyp[:, 0:1], A.mult, A.add))
    else:
        e_k0 = ev(vec.tensor_copy(T.key0[:], T.pidx[:]))
        wait(vec, e_key)
    wait(vec, e_km, e_m32)
    e_sb = ev(vec.tensor_scalar(T.sb[:], T.km[:], T.keyp[:, 0:1], None, A.is_equal))
    e_sf = ev(vec.tensor_scalar(T.sf[:], T.km[:], T.keyp[:, 0:1], None, A.is_equal))
    e_so = ev(vec.tensor_scalar(T.so[:], T.m32[:], T.keyp[:, 0:1], None, A.is_equal))
    wait(vec, e_k0)
    consts = [e_sb, e_sf, e_so]
    if rank == 0:
        consts.append(ev(vec.tensor_scalar(T.ex[:, 0:128], T.km[:], T.key0[:, 0:1], None, A.is_equal)))
        e_c = ev(vec.memset(T.cm[:], 0.0))
        wait(vec, e_c)
        for b in range(4):
            o = 128 * b + 32 * b
            consts.append(ev(vec.tensor_scalar(T.cm[:, o:o + 32], T.m32[:], T.key0[:, 0:1], None, A.is_equal)))
    else:
        for b in range(4):
            consts.append(ev(vec.tensor_scalar(T.ex[:, 128 * b:128 * b + 128], T.km[:], float(32 * b), T.key0[:, 0:1],
                                               A.add, A.is_equal)))
    wait(ten, *consts)

    wait(vec, e_hs)
    e_hf = ev(vec.tensor_copy(T.hsf[:], T.hsi[:]))
    wait(vec, e_hf)

    gathered = {}

    def hash_list(r):
        wait(vec, e_ids if r == rank else arrived(r, "ida%d" % r))
        a = ev(vec.tensor_scalar(slot(T.t1, r, L), slot(T.idl, r, L), T.hsf[:, 0:1], T.hsf[:, 1:2], A.mult, A.add))
        wait(vec, a)
        b = ev(vec.tensor_scalar(slot(T.t2, r, L), slot(T.t1, r, L), 4, 4095, A.logical_shift_right, A.bitwise_and))
        wait(vec, b)
        c = ev(vec.tensor_copy(slot(T.offs, r, L), slot(T.t2, r, L)))
        wait(vec, c)
        wait(act, c)
        if r == rank:
            wait(vec, e_mat)
            wait(act, e_mat)

    def gather(r, split):
        gathered[r] = {}
        for q, b0, b1 in split:
            dst = T.gat[:, r * K + b0 * C:r * K + b1 * C]
            src = T.win[:].indirect(T.offs[:, r * L + b0 * C // 16:r * L + b1 * C // 16])
            e = ev(vec.tensor_copy(dst, src) if q == "v" else act.activation(dst, src, ActivationFunctionType.Copy))
            for b in range(b0, b1):
                gathered[r][b] = e

    hash_list(rank)
    gather(rank, HALF)
    PA = [T["pa%d" % b] for b in range(NC)]
    PB = [T["pb%d" % b] for b in range(NC)]
    left, right = slice(0, C), slice(C, 2 * C)
    col = [slice(b * C, (b + 1) * C) for b in range(NC)]
    e_v0 = {}
    if rank == 0:
        for b in range(NC):
            wait(ten, gathered[0][b])
            e_v0[b] = ev(ten.matmul(PA[b][:, left], T.ex[:, 0:128], T.gat[:, col[b]], True, True))
        copies, packed = [], []

        def unload(i):
            r = SERVE[0][i]
            wait(vec, packed[i])
            e = ev(vec.tensor_copy(slot(T.c0s, r, 256), PB[i][:, 0:256]))
            copies.append(e)
            wait(g, e)
            send(r, T.c0l[:], slot(T.c0s, r, 256), "va")

        for i, r in enumerate(SERVE[0]):
            hash_list(r)
            gather(r, SPLIT[0])
            ins = None
            for b in range(NC):
                wait(ten, gathered[r][b])
                m = r * K + b * C
                ins = ten.matmul(PB[i][:, 0:256], T.cm[:, 128 * b:128 * b + 128], T.gat[:, m:m + C], b == 0, b == NC - 1)
            packed.append(ev(ins))
            if i:
                unload(i - 1)
        unload(N - 2)
        wait(ten, *copies)
    else:
        for r in SERVE[rank]:
            hash_list(r)
            gather(r, SPLIT[rank])
        relays = relays_of(core, T, topo)
        for i, (r, c0, c1, way) in enumerate(PLAN[rank]):
            wait(g, *sorted(set(gathered[r][b] for b in range(c0, c1))))
            m = slice(r * K + c0 * C, r * K + c1 * C)
            if way < 0:
                send(r, T.land[:, rank * K + c0 * C:rank * K + c1 * C], T.gat[:, m], "ma%d_%d" % (rank, c0))
            else:
                rid, pid, _se = topo.addr(relays[way])
                eng = inner_engines(core, relays[way], T.cores[r], topo)
                g.remote_dma(T.gat[:, m], T.gat[:, m], T.sem["rl%d" % i], T.sem["ls"], pid, rid, sum(1 << e for e in eng))
                sent[0] += len(eng)
        wait(ten, arrived(0, "va"))
        for b in range(NC):
            e_v0[b] = ev(ten.matmul(PA[b][:, left], T.ex[:, 128 * b:128 * b + 128], T.c0l[:], True, True))

    came = {}
    for q in PLAN:
        for r, c0, c1, way in PLAN[q]:
            if r == rank:
                src = T.cores[q] if way < 0 else relays_of(T.cores[q], T, topo)[way]
                for b in range(c0, c1):
                    came[q, b] = ("ma%d_%d" % (q, c0), len(topo.engines(src, core)))

    def picks(s, b):
        m = s * K + b * C
        if s == rank:
            return T.gat[:, m:m + C], gathered[rank][b]
        return T.land[:, m:m + C], came[s, b]

    e_hi, e_mm, e_fin = {}, {}, {}

    def m1(b):
        ap, e = picks(1, b)
        wait(vec, e_v0[b], e)
        if b in WHOLE[rank]:
            e = ev(vec.tensor_tensor(T.p1[:, col[b]], PA[b][:, left], ap, A.mult))
            wait(ten, e)
            e_mm[1, b] = ev(ten.matmul(PB[b][:, left], T.sf[:], T.p1[:, col[b]], True, True))
        else:
            e = ev(vec.tensor_tensor(PA[b][:, right], PA[b][:, left], ap, A.mult))
            wait(act, e)
            e_hi[b] = ev(act.activation(T.hi[:, col[b]], PA[b][:, right], ActivationFunctionType.Copy))

    def lo(b):
        wait(vec, e_hi[b])
        e = ev(vec.tensor_tensor(T.lo[:, col[b]], PA[b][:, right], T.hi[:, col[b]], A.subtract))
        wait(ten, e_hi[b])
        ten.matmul(PB[b][:, left], T.sb[:], T.hi[:, col[b]], True, False)
        wait(ten, e)
        e_mm[1, b] = ev(ten.matmul(PB[b][:, left], T.sb[:], T.lo[:, col[b]], False, True))

    def m2(b):
        ap, e = picks(2, b)
        wait(vec, e_mm[1, b], e)
        e = ev(vec.tensor_tensor(T.p2[:, col[b]], PB[b][:, left], ap, A.mult))
        wait(ten, e)
        e_mm[2, b] = ev(ten.matmul(PB[b][:, right], T.sf[:], T.p2[:, col[b]], True, True))

    def m3(b):
        ap, e = picks(3, b)
        wait(vec, e_mm[2, b], e)
        e = ev(vec.tensor_tensor(T.p3[:, col[b]], PB[b][:, right], ap, A.mult))
        wait(ten, e)
        e_fin[b] = [ev(ten.matmul(PA[b][:, 32 * j:32 * j + 32], T.p3[:, b * C + j:(b + 1) * C:2], T.so[:], True, True))
                    for j in range(2)]

    stored = []

    def out(b):
        wait(vec, *e_fin[b])
        for j in range(2):
            e = ev(vec.transpose(T.yb[:, 64 * b + j:64 * b + 64:2], PA[b][:, 32 * j:32 * j + 32]))
            wait(sync, e)
            wait(act, e)
        for a in range(4):
            q = act if a % 2 else sync
            o = b * C + 64 * a
            q.dma_start(T.y[:, o:o + 64], T.yb[32 * a:32 * a + 32, 64 * b:64 * b + 64]).then_inc(T.sem["st"], 16)
            stored.append(16)

    do = {"m1": m1, "lo": lo, "m2": m2, "m3": m3, "ou": out}
    for step in ORDER[rank].split():
        do[step[:2]](int(step[2]))
    wait(sync, ("st", sum(stored)))
    wait(g, ("ls", sent[0]))
